import numpy as np
import ml_dtypes


def mxq(x, axis, fmt="e4m3"):
    dtype, down = {"e4m3": (ml_dtypes.float8_e4m3fn, 7), "e5m2": (ml_dtypes.float8_e5m2, 14)}[fmt]
    v = np.moveaxis(np.asarray(x, np.float32).astype(ml_dtypes.bfloat16).astype(np.float64), axis, -1)
    blocks = v.reshape(v.shape[:-1] + (-1, 32))
    amax = np.abs(blocks).max(-1, keepdims=True)
    byte = np.maximum(np.where(amax > 0, np.frexp(amax)[1] - 1 + 127, 0) - down, 1)
    scale = np.exp2(byte - 127.0)
    codes = (blocks / scale).astype(np.float32).astype(dtype).astype(np.float64)
    return np.moveaxis((codes * scale).reshape(v.shape), -1, axis)


WIDE = False


def mx_kscale(k):
    if not WIDE:
        return np.ones(k)
    levels = np.array([10, -10, 5, -5, 0])
    if k % 512:
        return np.exp2(np.random.permutation(np.resize(levels, k // 32))).repeat(32)
    a = np.empty((k // 512, 16))
    for p in range(k // 512):
        a[p, :8] = np.random.permutation(np.resize(levels, 8))
        for g in range(8):
            far = levels[np.abs(levels - a[p, g]) >= 10]
            a[p, g + 8] = far[np.random.randint(len(far))]
    return np.exp2(a.ravel()).repeat(32)


def f64(x):
    return np.asarray(x).astype(np.float64)


def striped(idx):
    return np.tile(idx.reshape(-1, 16).T, (8, 1)).astype(np.uint16)


def unstriped(offs):
    return offs[:16].T.reshape(-1).astype(np.int64)


def pack_weight(w):
    k, n = w.shape
    w = f64(np.asarray(w, np.float32).astype(ml_dtypes.bfloat16)).reshape(k // 32, 32, n)
    amax = np.abs(w).max(1)
    byte = np.clip(np.where(amax > 0, np.frexp(amax)[1] - 1 + 127 - 7, 1), 1, 254)
    scaled = (w * np.exp2(127.0 - byte)[:, None, :]).reshape(k, n).astype(np.float32)
    words = np.ascontiguousarray(scaled.reshape(k // 512, 128, 4, n).transpose(0, 1, 3, 2)).astype(ml_dtypes.float8_e4m3fn).view(np.uint8)
    return words, np.ascontiguousarray(byte.astype(np.uint8).reshape(k // 512, 16, n))


def unpack_weight(words, scales):
    g, p, n, _ = words.shape
    vals = np.ascontiguousarray(words).view(ml_dtypes.float8_e4m3fn).astype(np.float64) * np.repeat(np.exp2(scales.astype(np.float64) - 127.0), 8, axis=1)[..., None]
    return vals.transpose(0, 1, 3, 2).reshape(g * 512, n)


K, T, E, C, N = 512, 2048, 16, 256, 128


def by_expert(wq, xq):
    return np.concatenate([wq[e].T @ xq[:, e * C:(e + 1) * C] for e in range(E)], axis=1)


def setup_inputs():
    n = np.random.standard_normal
    s = mx_kscale(K)[:, None]
    first = np.random.permutation(np.repeat(np.arange(E), T // E))
    second = (first + 1 + np.random.permutation(np.repeat(np.arange(E - 1), -(-T // (E - 1)))[:T])) % E
    while np.bincount(second, minlength=E).max() != T // E:
        load = np.bincount(second, minlength=E); hi, lo = int(load.argmax()), int(load.argmin())
        t = np.flatnonzero((second == hi) & (first != lo))[0]; second[t] = lo
    slot_token = np.empty(E * C, np.int64); pos = np.empty((2, T), np.int64); fill = np.zeros(E, np.int64)
    place = np.stack([np.random.permutation(C) for _ in range(E)])
    for r, deal in enumerate((first, second)):
        for t in np.random.permutation(T):
            e = deal[t]; j = e * C + place[e, fill[e]]; fill[e] += 1; slot_token[j] = t; pos[r, t] = j
    g = np.random.uniform(0.2, 0.8, T)
    packed = [pack_weight(m) for m in n((E, K, N)) / np.sqrt(K) / s[None]]
    return {
        "xT": (n((K, T)) * s).astype(np.float32),
        "w_words": np.stack([m[0] for m in packed]),
        "w_scales": np.stack([m[1] for m in packed]),
        "gate": np.stack([np.tile(g, (N, 1)), np.tile(1.0 - g, (N, 1))]).astype(np.float32),
        "offs": striped(slot_token),
        "pos1": striped(pos[0]),
        "pos2": striped(pos[1]),
    }


def reference(xT, w_words, w_scales, gate, offs, pos1, pos2):
    idx = unstriped(offs)
    xq = mxq(f64(xT)[:, idx], 0, "e4m3")
    w = np.stack([unpack_weight(w_words[e], w_scales[e]) for e in range(E)])
    y = by_expert(w, xq)
    return f64(gate[0]) * y[:, unstriped(pos1)] + f64(gate[1]) * y[:, unstriped(pos2)]

@@ -1,0 +1,144 @@
+from contextlib import ExitStack
+
+import concourse.mybir as mybir
+
+K, T, E, C, N = 512, 2048, 16, 256, 128
+SLOTS = E * C
+P = 128
+PACK = 4
+
+F32 = mybir.dt.float32
+BF16 = mybir.dt.bfloat16
+U32 = mybir.dt.uint32
+I32 = mybir.dt.int32
+U16 = mybir.dt.uint16
+U8 = mybir.dt.uint8
+FP8X4 = mybir.dt.float8_e4m3fn_x4
+MULT = mybir.AluOpType.mult
+ADD = mybir.AluOpType.add
+
+FLOPS = 2 * K * N * SLOTS
+
+CHUNKS = ((1024, 640), (768, 480), (256, 160))
+GATHERS = (1536, 1536, 768, 256)
+COMBINES = (1024, 640, 256, 128)
+
+
+def interleave(copy, grouped, raw, a, b):
+    if a < b:
+        copy(
+            grouped[:, a:b, :].rearrange("p (c i) t -> p c t i", i=4),
+            raw[:, :, a:b].rearrange("p t (c i) -> p c t i", i=4),
+        )
+
+
+def tile_routed_moe_kernel(tc, xT, w_words, w_scales, gate, offs, pos1, pos2, out):
+    nc = tc.nc
+    with ExitStack() as ctx:
+        keep = ctx.enter_context(tc.tile_pool(name="keep", bufs=1))
+        psum = ctx.enter_context(tc.psum_pool(name="psum", bufs=8))
+
+        offs_sb = keep.tile([P, SLOTS // 16], U16, name="offs_sb")
+        pos1_sb = keep.tile([P, T // 16], U16, name="pos1_sb")
+        pos2_sb = keep.tile([P, T // 16], U16, name="pos2_sb")
+
+        x_codes = keep.tile([P, T], U32, name="x_codes", align_bytes=64)
+        x_scales = keep.tile([P, T], U8, name="x_scales", align_bytes=64)
+        g_codes = keep.tile([P, SLOTS], U32, name="g_codes", align_bytes=64)
+        g_scales = keep.tile([P, SLOTS], U8, name="g_scales", align_bytes=64)
+        w_codes = keep.tile([P, E, N], U32, name="w_codes", align_bytes=64)
+        w_bytes = keep.tile([P, E * N], U8, name="w_bytes", align_bytes=64)
+        y = keep.tile([P, SLOTS], F32, name="y")
+        gate_sb = keep.tile([P, 2, T], F32, name="gate_sb")
+
+        nc.gpsimd.memset(x_scales[:], 0)
+        nc.vector.memset(w_bytes[:].bitcast(I32), 0)
+
+        x_view = xT.rearrange("(p t) n -> p t n", t=PACK)
+        raws = []
+        t0 = 0
+        for i, (n, n_vec) in enumerate(CHUNKS):
+            raw = keep.tile([P, PACK, n], F32, name=f"raw{i}")
+            nc.sync.dma_start(out=raw[:], in_=x_view[:, :, t0 : t0 + n])
+            raws.append(raw)
+            t0 += n
+        nc.sync.dma_start(offs_sb[:], offs)
+        for q in range(4):
+            nc.sync.dma_start(
+                out=w_bytes[32 * q : 32 * q + 4, :].rearrange("q (e n) -> q e n", e=E).bitcast(I32),
+                in_=w_scales.rearrange("e a q n -> q (e a) n")[4 * q : 4 * q + 4].bitcast(I32),
+            )
+        nc.sync.dma_start(
+            out=w_codes[:].bitcast(I32),
+            in_=w_words.rearrange("e a p n r -> p (e a) (n r)").bitcast(I32),
+        )
+        nc.sync.dma_start(pos1_sb[:], pos1)
+        nc.sync.dma_start(pos2_sb[:], pos2)
+        nc.sync.dma_start(out=gate_sb[:], in_=gate.rearrange("g p t -> p g t"))
+
+        t0 = 0
+        for i, (n, n_vec) in enumerate(CHUNKS):
+            grouped = keep.tile([P, n, PACK], BF16, name=f"grouped{i}", align_bytes=64)
+            interleave(nc.vector.tensor_copy, grouped, raws[i], 0, n_vec)
+            interleave(nc.scalar.copy, grouped, raws[i], n_vec, n)
+            a = 0
+            while a < n:
+                m = 512 if n - a >= 512 else 256
+                nc.vector.quantize_mx(
+                    out=x_codes[:, t0 + a : t0 + a + m].bitcast(FP8X4),
+                    scales=x_scales[:, t0 + a : t0 + a + m],
+                    in_=grouped[:, a : a + m, :].rearrange("p n t -> p (n t)"),
+                )
+                a += m
+            t0 += n
+
+        s0 = 0
+        bank = None
+        for n in GATHERS:
+            cols = slice(s0, s0 + n)
+            lst = offs_sb[:, s0 // 16 : (s0 + n) // 16]
+            nc.vector.tensor_copy(g_codes[:, cols], x_codes[:].indirect(lst))
+            nc.vector.tensor_copy(g_scales[:, cols], x_scales[:].indirect(lst))
+            for e in range(s0 // C, (s0 + n) // C):
+                if e % 2 == 0:
+                    bank = psum.tile([P, 2 * C], F32, name="bank")
+                h = (e % 2) * C
+                slots = slice(e * C, (e + 1) * C)
+                nc.tensor.matmul_mx(
+                    out=bank[:, h : h + C],
+                    lhsT=w_codes[:, e, :].bitcast(FP8X4),
+                    lhsT_scale=w_bytes[:, e * N : (e + 1) * N],
+                    rhs=g_codes[:, slots].bitcast(FP8X4),
+                    rhs_scale=g_scales[:, slots],
+                    start=True,
+                    stop=True,
+                )
+                if e % 2 == 1:
+                    nc.scalar.copy(y[:, (e - 1) * C : (e + 1) * C], bank[:])
+            s0 += n
+
+        first = keep.tile([P, T], F32, name="first")
+        second = keep.tile([P, T], F32, name="second")
+        result = keep.tile([P, T], F32, name="result")
+
+        def pick(dst, positions, g, a, b):
+            nc.vector.tensor_tensor(
+                dst[:, a:b], y[:].indirect(positions[:, a // 16 : b // 16]), gate_sb[:, g, a:b], MULT
+            )
+
+        def finish(a, b):
+            nc.vector.tensor_tensor(result[:, a:b], first[:, a:b], second[:, a:b], ADD)
+            nc.sync.dma_start(out=out[:, a:b], in_=result[:, a:b])
+
+        edges = [0]
+        for n in COMBINES:
+            edges.append(edges[-1] + n)
+        last = len(COMBINES) - 1
+        for i in range(last + 1):
+            a, b = edges[i], edges[i + 1]
+            pick(first, pos1_sb, 0, a, b)
+            if 0 < i < last:
+                finish(edges[i - 1], a)
+            pick(second, pos2_sb, 1, a, b)
+        finish(edges[last - 1], edges[last])
+        finish(edges[last], T)

@@ -1,6 +1,7 @@
 from contextlib import ExitStack
 
 import concourse.mybir as mybir
+from concourse.masks import make_identity
 
 K, T, E, C, N = 512, 2048, 16, 256, 128
 SLOTS = E * C
@@ -20,8 +21,9 @@ ADD = mybir.AluOpType.add
 FLOPS = 2 * K * N * SLOTS
 
 CHUNKS = ((1024, 640), (768, 480), (256, 160))
-GATHERS = (1536, 1536, 768, 256)
-COMBINES = (1024, 640, 256, 128)
+GATHERS = ((1536, 1536), (1536, 1536), (768, 1024), (256, 0))
+COMBINES = (512, 256, 512, 384, 256, 128)
+ADDERS = "TTVVVV"
 
 
 def interleave(copy, grouped, raw, a, b):
@@ -52,6 +54,8 @@ def tile_routed_moe_kernel(tc, xT, w_words, w_scales, gate, offs, pos1, pos2, ou
         gate_sb = keep.tile([P, 2, T], F32, name="gate_sb")
 
         nc.gpsimd.memset(x_scales[:], 0)
+        ident = keep.tile([P, P], F32, name="ident")
+        make_identity(nc, ident[:])
         nc.vector.memset(w_bytes[:].bitcast(I32), 0)
 
         x_view = xT.rearrange("(p t) n -> p t n", t=PACK)
@@ -83,7 +87,9 @@ def tile_routed_moe_kernel(tc, xT, w_words, w_scales, gate, offs, pos1, pos2, ou
             interleave(nc.scalar.copy, grouped, raws[i], n_vec, n)
             a = 0
             while a < n:
-                m = 512 if n - a >= 512 else 256
+                m = 512
+                while m > n - a:
+                    m //= 2
                 nc.vector.quantize_mx(
                     out=x_codes[:, t0 + a : t0 + a + m].bitcast(FP8X4),
                     scales=x_scales[:, t0 + a : t0 + a + m],
@@ -92,53 +98,88 @@ def tile_routed_moe_kernel(tc, xT, w_words, w_scales, gate, offs, pos1, pos2, ou
                 a += m
             t0 += n
 
+        def multiply(dst, e, a, b):
+            slots = slice(e * C + a, e * C + b)
+            nc.tensor.matmul_mx(
+                out=dst,
+                lhsT=w_codes[:, e, :].bitcast(FP8X4),
+                lhsT_scale=w_bytes[:, e * N : (e + 1) * N],
+                rhs=g_codes[:, slots].bitcast(FP8X4),
+                rhs_scale=g_scales[:, slots],
+                start=True,
+                stop=True,
+            )
+
         s0 = 0
-        bank = None
-        for n in GATHERS:
-            cols = slice(s0, s0 + n)
-            lst = offs_sb[:, s0 // 16 : (s0 + n) // 16]
-            nc.vector.tensor_copy(g_codes[:, cols], x_codes[:].indirect(lst))
-            nc.vector.tensor_copy(g_scales[:, cols], x_scales[:].indirect(lst))
-            for e in range(s0 // C, (s0 + n) // C):
-                if e % 2 == 0:
-                    bank = psum.tile([P, 2 * C], F32, name="bank")
-                h = (e % 2) * C
-                slots = slice(e * C, (e + 1) * C)
-                nc.tensor.matmul_mx(
-                    out=bank[:, h : h + C],
-                    lhsT=w_codes[:, e, :].bitcast(FP8X4),
-                    lhsT_scale=w_bytes[:, e * N : (e + 1) * N],
-                    rhs=g_codes[:, slots].bitcast(FP8X4),
-                    rhs_scale=g_scales[:, slots],
-                    start=True,
-                    stop=True,
+        for n, n_codes in GATHERS:
+            if n_codes:
+                nc.vector.tensor_copy(
+                    g_codes[:, s0 : s0 + n_codes], x_codes[:].indirect(offs_sb[:, s0 // 16 : (s0 + n_codes) // 16])
                 )
-                if e % 2 == 1:
-                    nc.scalar.copy(y[:, (e - 1) * C : (e + 1) * C], bank[:])
+            nc.vector.tensor_copy(g_scales[:, s0 : s0 + n], x_scales[:].indirect(offs_sb[:, s0 // 16 : (s0 + n) // 16]))
+            e = s0 // C
             s0 += n
+            while e < s0 // C:
+                if e == E - 1:
+                    for a, copy in ((0, nc.scalar.copy), (C // 2, nc.vector.tensor_copy)):
+                        bank = psum.tile([P, 2 * C], F32, name="bank")
+                        multiply(bank[:, 0 : C // 2], e, a, a + C // 2)
+                        copy(y[:, e * C + a : e * C + a + C // 2], bank[:, 0 : C // 2])
+                    e += 1
+                    continue
+                bank = psum.tile([P, 2 * C], F32, name="bank")
+                m = min(2, s0 // C - e)
+                for h in range(m):
+                    multiply(bank[:, h * C : (h + 1) * C], e + h, 0, C)
+                nc.scalar.copy(y[:, e * C : (e + m) * C], bank[:, 0 : m * C])
+                e += m
 
         first = keep.tile([P, T], F32, name="first")
         second = keep.tile([P, T], F32, name="second")
         result = keep.tile([P, T], F32, name="result")
+        total = keep.tile([P, T], F32, name="total")
 
         def pick(dst, positions, g, a, b):
             nc.vector.tensor_tensor(
                 dst[:, a:b], y[:].indirect(positions[:, a // 16 : b // 16]), gate_sb[:, g, a:b], MULT
             )
 
-        def finish(a, b):
-            nc.vector.tensor_tensor(result[:, a:b], first[:, a:b], second[:, a:b], ADD)
+        def finish(i):
+            a, b = edges[i], edges[i + 1]
+            if ADDERS[i] == "M":
+                bank = psum.tile([P, 2 * C], F32, name="bank")
+                nc.tensor.matmul(bank[:, 0 : b - a], ident[:], first[:, a:b], start=True, stop=False)
+                nc.tensor.matmul(bank[:, 0 : b - a], ident[:], second[:, a:b], start=False, stop=True)
+                nc.scalar.copy(result[:, a:b], bank[:, 0 : b - a])
+            elif ADDERS[i] == "T":
+                turned = psum.tile([P, 2 * C], F32, name="bank")
+                for c in range(0, b - a, P):
+                    blk = slice(a + c, a + c + P)
+                    dst = turned[:, c : c + P]
+                    nc.tensor.matmul(dst, first[:, blk], ident[:], start=True, stop=False, is_transpose=True)
+                    nc.tensor.matmul(dst, second[:, blk], ident[:], start=False, stop=True, is_transpose=True)
+                nc.scalar.copy(total[:, a:b], turned[:, 0 : b - a])
+                back = psum.tile([P, 2 * C], F32, name="bank")
+                for c in range(0, b - a, P):
+                    nc.tensor.transpose(back[:, c : c + P], total[:, a + c : a + c + P], ident[:])
+                nc.scalar.copy(result[:, a:b], back[:, 0 : b - a])
+            else:
+                nc.vector.tensor_tensor(result[:, a:b], first[:, a:b], second[:, a:b], ADD)
             nc.sync.dma_start(out=out[:, a:b], in_=result[:, a:b])
 
         edges = [0]
         for n in COMBINES:
             edges.append(edges[-1] + n)
         last = len(COMBINES) - 1
+        n_tensor = ADDERS.index("V")
         for i in range(last + 1):
             a, b = edges[i], edges[i + 1]
-            pick(first, pos1_sb, 0, a, b)
-            if 0 < i < last:
-                finish(edges[i - 1], a)
+            if i < n_tensor:
+                pick(first, pos1_sb, 0, a, b)
+            elif i == n_tensor:
+                pick(first, pos1_sb, 0, a, T)
             pick(second, pos2_sb, 1, a, b)
-        finish(edges[last - 1], edges[last])
-        finish(edges[last], T)
+            if 0 < i < last:
+                finish(i - 1)
+        finish(last - 1)
+        finish(last)

@@ -21,7 +21,7 @@ ADD = mybir.AluOpType.add
 FLOPS = 2 * K * N * SLOTS
 
 CHUNKS = ((1024, 640), (768, 480), (256, 160))
-GATHERS = ((1536, 1536), (1536, 1536), (768, 1024), (256, 0))
+GATHERS = ((1536, 1536), (1536, 1536), (512, 1024), (256, 0), (256, 0))
 COMBINES = (512, 256, 512, 384, 256, 128)
 ADDERS = "TTVVVV"
 

from contextlib import ExitStack

import concourse.mybir as mybir
from concourse.masks import make_identity

K, T, E, C, N = 512, 2048, 16, 256, 128
SLOTS = E * C
P = 128
PACK = 4

F32 = mybir.dt.float32
BF16 = mybir.dt.bfloat16
U32 = mybir.dt.uint32
I32 = mybir.dt.int32
U16 = mybir.dt.uint16
U8 = mybir.dt.uint8
FP8X4 = mybir.dt.float8_e4m3fn_x4
MULT = mybir.AluOpType.mult
ADD = mybir.AluOpType.add

FLOPS = 2 * K * N * SLOTS

CHUNKS = ((1024, 640), (768, 480), (256, 160))
GATHERS = ((1536, 1536), (1536, 1536), (512, 1024), (256, 0), (256, 0))
COMBINES = (512, 256, 512, 384, 256, 128)
ADDERS = "TTVVVV"


def interleave(copy, grouped, raw, a, b):
    if a < b:
        copy(
            grouped[:, a:b, :].rearrange("p (c i) t -> p c t i", i=4),
            raw[:, :, a:b].rearrange("p t (c i) -> p c t i", i=4),
        )


def tile_routed_moe_kernel(tc, xT, w_words, w_scales, gate, offs, pos1, pos2, out):
    nc = tc.nc
    with ExitStack() as ctx:
        keep = ctx.enter_context(tc.tile_pool(name="keep", bufs=1))
        psum = ctx.enter_context(tc.psum_pool(name="psum", bufs=8))

        offs_sb = keep.tile([P, SLOTS // 16], U16, name="offs_sb")
        pos1_sb = keep.tile([P, T // 16], U16, name="pos1_sb")
        pos2_sb = keep.tile([P, T // 16], U16, name="pos2_sb")

        x_codes = keep.tile([P, T], U32, name="x_codes", align_bytes=64)
        x_scales = keep.tile([P, T], U8, name="x_scales", align_bytes=64)
        g_codes = keep.tile([P, SLOTS], U32, name="g_codes", align_bytes=64)
        g_scales = keep.tile([P, SLOTS], U8, name="g_scales", align_bytes=64)
        w_codes = keep.tile([P, E, N], U32, name="w_codes", align_bytes=64)
        w_bytes = keep.tile([P, E * N], U8, name="w_bytes", align_bytes=64)
        y = keep.tile([P, SLOTS], F32, name="y")
        gate_sb = keep.tile([P, 2, T], F32, name="gate_sb")

        nc.gpsimd.memset(x_scales[:], 0)
        ident = keep.tile([P, P], F32, name="ident")
        make_identity(nc, ident[:])
        nc.vector.memset(w_bytes[:].bitcast(I32), 0)

        x_view = xT.rearrange("(p t) n -> p t n", t=PACK)
        raws = []
        t0 = 0
        for i, (n, n_vec) in enumerate(CHUNKS):
            raw = keep.tile([P, PACK, n], F32, name=f"raw{i}")
            nc.sync.dma_start(out=raw[:], in_=x_view[:, :, t0 : t0 + n])
            raws.append(raw)
            t0 += n
        nc.sync.dma_start(offs_sb[:], offs)
        for q in range(4):
            nc.sync.dma_start(
                out=w_bytes[32 * q : 32 * q + 4, :].rearrange("q (e n) -> q e n", e=E).bitcast(I32),
                in_=w_scales.rearrange("e a q n -> q (e a) n")[4 * q : 4 * q + 4].bitcast(I32),
            )
        nc.sync.dma_start(
            out=w_codes[:].bitcast(I32),
            in_=w_words.rearrange("e a p n r -> p (e a) (n r)").bitcast(I32),
        )
        nc.sync.dma_start(pos1_sb[:], pos1)
        nc.sync.dma_start(pos2_sb[:], pos2)
        nc.sync.dma_start(out=gate_sb[:], in_=gate.rearrange("g p t -> p g t"))

        t0 = 0
        for i, (n, n_vec) in enumerate(CHUNKS):
            grouped = keep.tile([P, n, PACK], BF16, name=f"grouped{i}", align_bytes=64)
            interleave(nc.vector.tensor_copy, grouped, raws[i], 0, n_vec)
            interleave(nc.scalar.copy, grouped, raws[i], n_vec, n)
            a = 0
            while a < n:
                m = 512
                while m > n - a:
                    m //= 2
                nc.vector.quantize_mx(
                    out=x_codes[:, t0 + a : t0 + a + m].bitcast(FP8X4),
                    scales=x_scales[:, t0 + a : t0 + a + m],
                    in_=grouped[:, a : a + m, :].rearrange("p n t -> p (n t)"),
                )
                a += m
            t0 += n

        def multiply(dst, e, a, b):
            slots = slice(e * C + a, e * C + b)
            nc.tensor.matmul_mx(
                out=dst,
                lhsT=w_codes[:, e, :].bitcast(FP8X4),
                lhsT_scale=w_bytes[:, e * N : (e + 1) * N],
                rhs=g_codes[:, slots].bitcast(FP8X4),
                rhs_scale=g_scales[:, slots],
                start=True,
                stop=True,
            )

        s0 = 0
        for n, n_codes in GATHERS:
            if n_codes:
                nc.vector.tensor_copy(
                    g_codes[:, s0 : s0 + n_codes], x_codes[:].indirect(offs_sb[:, s0 // 16 : (s0 + n_codes) // 16])
                )
            nc.vector.tensor_copy(g_scales[:, s0 : s0 + n], x_scales[:].indirect(offs_sb[:, s0 // 16 : (s0 + n) // 16]))
            e = s0 // C
            s0 += n
            while e < s0 // C:
                if e == E - 1:
                    for a, copy in ((0, nc.scalar.copy), (C // 2, nc.vector.tensor_copy)):
                        bank = psum.tile([P, 2 * C], F32, name="bank")
                        multiply(bank[:, 0 : C // 2], e, a, a + C // 2)
                        copy(y[:, e * C + a : e * C + a + C // 2], bank[:, 0 : C // 2])
                    e += 1
                    continue
                bank = psum.tile([P, 2 * C], F32, name="bank")
                m = min(2, s0 // C - e)
                for h in range(m):
                    multiply(bank[:, h * C : (h + 1) * C], e + h, 0, C)
                nc.scalar.copy(y[:, e * C : (e + m) * C], bank[:, 0 : m * C])
                e += m

        first = keep.tile([P, T], F32, name="first")
        second = keep.tile([P, T], F32, name="second")
        result = keep.tile([P, T], F32, name="result")
        total = keep.tile([P, T], F32, name="total")

        def pick(dst, positions, g, a, b):
            nc.vector.tensor_tensor(
                dst[:, a:b], y[:].indirect(positions[:, a // 16 : b // 16]), gate_sb[:, g, a:b], MULT
            )

        def finish(i):
            a, b = edges[i], edges[i + 1]
            if ADDERS[i] == "M":
                bank = psum.tile([P, 2 * C], F32, name="bank")
                nc.tensor.matmul(bank[:, 0 : b - a], ident[:], first[:, a:b], start=True, stop=False)
                nc.tensor.matmul(bank[:, 0 : b - a], ident[:], second[:, a:b], start=False, stop=True)
                nc.scalar.copy(result[:, a:b], bank[:, 0 : b - a])
            elif ADDERS[i] == "T":
                turned = psum.tile([P, 2 * C], F32, name="bank")
                for c in range(0, b - a, P):
                    blk = slice(a + c, a + c + P)
                    dst = turned[:, c : c + P]
                    nc.tensor.matmul(dst, first[:, blk], ident[:], start=True, stop=False, is_transpose=True)
                    nc.tensor.matmul(dst, second[:, blk], ident[:], start=False, stop=True, is_transpose=True)
                nc.scalar.copy(total[:, a:b], turned[:, 0 : b - a])
                back = psum.tile([P, 2 * C], F32, name="bank")
                for c in range(0, b - a, P):
                    nc.tensor.transpose(back[:, c : c + P], total[:, a + c : a + c + P], ident[:])
                nc.scalar.copy(result[:, a:b], back[:, 0 : b - a])
            else:
                nc.vector.tensor_tensor(result[:, a:b], first[:, a:b], second[:, a:b], ADD)
            nc.sync.dma_start(out=out[:, a:b], in_=result[:, a:b])

        edges = [0]
        for n in COMBINES:
            edges.append(edges[-1] + n)
        last = len(COMBINES) - 1
        n_tensor = ADDERS.index("V")
        for i in range(last + 1):
            a, b = edges[i], edges[i + 1]
            if i < n_tensor:
                pick(first, pos1_sb, 0, a, b)
            elif i == n_tensor:
                pick(first, pos1_sb, 0, a, T)
            pick(second, pos2_sb, 1, a, b)
            if 0 < i < last:
                finish(i - 1)
        finish(last - 1)
        finish(last)
